import numpy as np
import ml_dtypes


def mxq(x, axis, fmt="e4m3"):
    dtype, down = {"e4m3": (ml_dtypes.float8_e4m3fn, 7), "e5m2": (ml_dtypes.float8_e5m2, 14)}[fmt]
    v = np.moveaxis(np.asarray(x, np.float32).astype(ml_dtypes.bfloat16).astype(np.float64), axis, -1)
    blocks = v.reshape(v.shape[:-1] + (-1, 32))
    amax = np.abs(blocks).max(-1, keepdims=True)
    byte = np.maximum(np.where(amax > 0, np.frexp(amax)[1] - 1 + 127, 0) - down, 1)
    scale = np.exp2(byte - 127.0)
    codes = (blocks / scale).astype(np.float32).astype(dtype).astype(np.float64)
    return np.moveaxis((codes * scale).reshape(v.shape), -1, axis)


WIDE = False


def mx_kscale(k):
    if not WIDE:
        return np.ones(k)
    levels = np.array([10, -10, 5, -5, 0])
    if k % 512:
        return np.exp2(np.random.permutation(np.resize(levels, k // 32))).repeat(32)
    a = np.empty((k // 512, 16))
    for p in range(k // 512):
        a[p, :8] = np.random.permutation(np.resize(levels, 8))
        for g in range(8):
            far = levels[np.abs(levels - a[p, g]) >= 10]
            a[p, g + 8] = far[np.random.randint(len(far))]
    return np.exp2(a.ravel()).repeat(32)


def f64(x):
    return np.asarray(x).astype(np.float64)


def striped(idx):
    return np.tile(np.asarray(idx).reshape(-1, 16).T, (8, 1)).astype(np.uint16)


def unstriped(offs):
    return offs[:16].T.reshape(-1).astype(np.int64)


E2M1 = np.array([0.0, 0.5, 1.0, 1.5, 2.0, 3.0, 4.0, 6.0, -0.0, -0.5, -1.0, -1.5, -2.0, -3.0, -4.0, -6.0])


def pack_weight(w, fmt):
    k, n = w.shape
    w = f64(np.asarray(w, np.float32).astype(ml_dtypes.bfloat16)).reshape(k // 32, 32, n)
    amax = np.abs(w).max(1)
    if fmt == "e4m3":
        byte = np.frexp(amax)[1] - 1 + 127 - 7
    else:
        mant, ex = np.frexp(amax / 6.0)
        byte = np.where(mant > 0.5, ex, ex - 1) + 127
    byte = np.clip(np.where(amax > 0, byte, 1), 1, 254)
    scaled = (w * np.exp2(127.0 - byte)[:, None, :]).reshape(k, n).astype(np.float32)
    by_word = np.ascontiguousarray(scaled.reshape(k // 512, 128, 4, n).transpose(0, 1, 3, 2))
    if fmt == "e4m3":
        words = by_word.astype(ml_dtypes.float8_e4m3fn).view(np.uint8)
    else:
        c = by_word.astype(ml_dtypes.float4_e2m1fn).view(np.uint8) & 0xF
        words = (c[..., 0::2] | (c[..., 1::2] << 4)).reshape(k // 512, 128, 2 * n)
    return np.ascontiguousarray(words), np.ascontiguousarray(byte.astype(np.uint8).reshape(k // 512, 16, n))


def unpack_weight(words, scales, fmt):
    g, _, n = scales.shape
    words = np.ascontiguousarray(words).reshape(g, 128, n, -1)
    if fmt == "e4m3":
        vals = words.view(ml_dtypes.float8_e4m3fn).astype(np.float64)
    else:
        nib = np.empty((g, 128, n, 4), np.uint8)
        nib[..., 0::2] = words & 0xF
        nib[..., 1::2] = words >> 4
        vals = E2M1[nib]
    vals = vals * np.repeat(np.exp2(scales.astype(np.float64) - 127.0), 8, axis=1)[..., None]
    return vals.transpose(0, 1, 3, 2).reshape(g * 512, n)


D, T, I, Q, E, Z = 512, 2048, 512, 128, 512, 1024


def setup_inputs():
    n = np.random.standard_normal
    idx = np.random.permutation(T)[:I]
    idx2 = np.random.permutation(Z)[:I]
    idx3 = np.random.permutation(Z)[:I]
    fd = mx_kscale(D)
    fi = mx_kscale(I)
    ti = np.ones(T)
    ti[idx] = fi
    keysp = pack_weight(n((D, T)) / fd[:, None], "e4m3")
    return {
        "query": (n((D, Q)) * 1.0 / np.sqrt(D) * fd[:, None]).astype(np.float32),
        "keys_words": keysp[0],
        "keys_scales": keysp[1],
        "os": (np.random.uniform(0.02, 0.08, (1, I)) * fi).astype(np.float32),
        "vals": (n((E, T)) / ti).astype(np.float32),
        "offs": striped(idx),
        "offs2": striped(idx2),
        "offs3": striped(idx3),
    }


def reference(query, keys_words, keys_scales, os, vals, offs, offs2, offs3):
    idx = unstriped(offs)
    idx2 = unstriped(offs2)
    idx3 = unstriped(offs3)
    keysu = unpack_weight(keys_words, keys_scales, "e4m3")
    queryq = mxq(f64(query), 0, "e4m3")
    keysidxg = keysu[:, idx]
    a = queryq.T @ keysidxg
    f0 = np.zeros((Q, Z))
    f0[:, idx2] = a
    s = a + f0[:, idx3]
    w = np.maximum(s, 0.0)
    wo1 = w * f64(os)
    wt1 = wo1.T
    vt1 = f64(vals)[:, idx].T
    wt1q = mxq(wt1, 0, "e4m3")
    vt1q = mxq(vt1, 0, "e4m3")
    o = wt1q.T @ vt1q
    return o

@@ -1,0 +1,210 @@
+from contextlib import ExitStack
+
+import concourse.mybir as mybir
+from concourse.masks import make_identity
+
+D, T, I, Q, E, Z = 512, 2048, 512, 128, 512, 1024
+FLOPS = 2 * Q * D * I + 2 * Q * I * E
+
+F32 = mybir.dt.float32
+BF16 = mybir.dt.bfloat16
+I32 = mybir.dt.int32
+U32 = mybir.dt.uint32
+U16 = mybir.dt.uint16
+U8 = mybir.dt.uint8
+FP8X4 = mybir.dt.float8_e4m3fn_x4
+COPY = mybir.ActivationFunctionType.Copy
+ALU = mybir.AluOpType
+
+P = 128
+PACK = 4
+HALF = I // 2
+LIST_COLS = I // 16
+BLOCKS = E // P
+SHARE = 320
+
+
+def tile_attend_passedthrough_read_lean_kernel(tc, query, keys_words, keys_scales, factors, vals, offs, offs2, offs3, out):
+    nc = tc.nc
+    with ExitStack() as ctx:
+        lists = ctx.enter_context(tc.tile_pool(name="lists", bufs=1))
+        keep = ctx.enter_context(tc.tile_pool(name="keep", bufs=1))
+        psum = ctx.enter_context(tc.psum_pool(name="psum", bufs=1))
+
+        token_list = lists.tile([P, LIST_COLS], U16, name="token_list")
+        put_list = lists.tile([P, LIST_COLS], U16, name="put_list")
+        take_list = lists.tile([P, LIST_COLS], U16, name="take_list")
+
+        def half_of(list_tile, h):
+            return list_tile[:, h * LIST_COLS // 2 : (h + 1) * LIST_COLS // 2]
+
+        key_words = keep.tile([P, T], U32, name="key_words", tag="slot3", align_bytes=64)
+        key_bytes = keep.tile([P, T], U8, name="key_bytes", tag="slot2", align_bytes=64)
+        query_raw = keep.tile([P, PACK, Q], F32, name="query_raw", tag="slot0", align_bytes=64)
+        slot_factor = keep.tile([P, PACK], F32, name="slot_factor", tag="listed3")
+        places = keep.tile([P, Z], F32, name="places")
+        identity = keep.tile([P, P], F32, name="identity")
+
+        nc.vector.memset(key_bytes[:].bitcast(I32), 0)
+        nc.sync.dma_start(token_list[:], offs)
+        nc.sync.dma_start(out=query_raw[:], in_=query.rearrange("(p j) q -> p j q", j=PACK))
+        nc.sync.dma_start(
+            out=key_words[:].bitcast(I32), in_=keys_words[0].rearrange("p n t -> p (n t)").bitcast(I32)
+        )
+        nc.sync.dma_start(put_list[:], offs2)
+        for r in range(4):
+            nc.scalar.dma_start(
+                out=key_bytes[r:P:32, :].bitcast(I32), in_=keys_scales[0][r:16:4, :].bitcast(I32)
+            )
+        nc.sync.dma_start(take_list[:], offs3)
+        nc.gpsimd.dma_start(out=slot_factor[:], in_=factors.rearrange("o (p t) -> (o p) t", t=PACK))
+        nc.vector.memset(places[:], 0.0)
+        make_identity(nc, identity[:])
+
+        query_grouped = keep.tile([P, Q, PACK], BF16, name="query_grouped", tag="slot1", align_bytes=64)
+        query_codes = keep.tile([P, Q], U32, name="query_codes", align_bytes=64)
+        query_scales = keep.tile([P, Q], U8, name="query_scales", align_bytes=64)
+        nc.vector.tensor_copy(query_grouped[:], query_raw[:].rearrange("p j q -> p q j"))
+        nc.vector.quantize_mx(
+            out=query_codes[:].bitcast(FP8X4),
+            scales=query_scales[:],
+            in_=query_grouped[:].rearrange("p q j -> p (q j)"),
+        )
+
+        listed_words = keep.tile([P, I], U32, name="listed_words", align_bytes=64)
+        listed_bytes = keep.tile([P, I], U8, name="listed_bytes", align_bytes=64)
+        nc.vector.tensor_copy(listed_bytes[:], key_bytes[:].indirect(token_list[:]))
+        products = keep.tile([P, I], F32, name="products")
+        for h in range(2):
+            cols = slice(h * HALF, (h + 1) * HALF)
+            nc.vector.tensor_copy(listed_words[:, cols], key_words[:].indirect(half_of(token_list, h)))
+        value_pool = []
+        for b in range(BLOCKS):
+            pool_block = keep.tile([P, T], F32, name=f"value_pool{b}", tag=f"slot{b}", align_bytes=64)
+            nc.sync.dma_start(out=pool_block[:], in_=vals[b * P : (b + 1) * P, :])
+            value_pool.append(pool_block)
+        for h in range(2):
+            cols = slice(h * HALF, (h + 1) * HALF)
+            bank = psum.tile([P, HALF], F32, name=f"product_bank{h}", tag=f"acc{h}")
+            nc.tensor.matmul_mx(
+                out=bank[:],
+                lhsT=query_codes[:].bitcast(FP8X4),
+                lhsT_scale=query_scales[:],
+                rhs=listed_words[:, cols].bitcast(FP8X4),
+                rhs_scale=listed_bytes[:, cols],
+                start=True,
+                stop=True,
+            )
+            if h == 0:
+                nc.scalar.activation(products[:, cols], bank[:], COPY)
+            else:
+                nc.vector.tensor_copy(products[:, cols], bank[:])
+            nc.scalar.activation(places[:].indirect(half_of(put_list, h)), products[:, cols], COPY)
+
+        scores_t = psum.tile([P, PACK, Q], F32, name="scores_t")
+        for t in range(PACK):
+            nc.tensor.matmul(
+                scores_t[:, t, :], lhsT=products[:, t:I:PACK], rhs=identity[:],
+                is_transpose=True, start=(t == 0), stop=False,
+            )
+
+        last = BLOCKS - 1
+        listed_values = [keep.tile([P, I], BF16, name=f"listed_values{b}", tag=f"listed{b}") for b in range(last)]
+        value_grouped = keep.tile([P, E * PACK], BF16, name="value_grouped", align_bytes=64)
+        value_codes = keep.tile([P, E], U32, name="value_codes", align_bytes=64)
+        value_scales = keep.tile([P, E], U8, name="value_scales", align_bytes=64)
+        value_banks = [psum.tile([P, 2, P], F32, name=f"value_bank{b}") for b in range(BLOCKS)]
+
+        def gather_on_vector(dst, window, offsets):
+            nc.vector.tensor_copy(dst, window.indirect(offsets))
+
+        def gather_on_scalar(dst, window, offsets):
+            nc.scalar.activation(dst, window.indirect(offsets), COPY)
+
+        def turn_values(b):
+            words = listed_values[b][:].bitcast(F32)
+            for u in range(2):
+                nc.tensor.transpose(value_banks[b][:, u, :], words[:, u : I // 2 : 2], identity[:])
+
+        def group_values(b, copy):
+            copy(
+                value_grouped[:, b * P * PACK : (b + 1) * P * PACK].bitcast(F32).rearrange("p (e u) -> p e u", u=2),
+                value_banks[b][:].rearrange("p u e -> p e u"),
+            )
+
+        def quantize_values(first, count):
+            cols = slice(first * P, (first + count) * P)
+            nc.vector.quantize_mx(
+                out=value_codes[:, cols].bitcast(FP8X4),
+                scales=value_scales[:, cols],
+                in_=value_grouped[:, cols.start * PACK : cols.stop * PACK],
+            )
+
+        gather_on_vector(listed_values[0][:], value_pool[0][:], token_list[:])
+        turn_values(0)
+        group_values(0, nc.vector.tensor_copy)
+        quantize_values(0, 1)
+
+        gather_on_vector(listed_values[1][:], value_pool[1][:], token_list[:])
+        turn_values(1)
+        looked_up = keep.tile([P, I], F32, name="looked_up", tag="slot1", align_bytes=64)
+        gather_on_vector(looked_up[:, :SHARE], places[:], take_list[:, : SHARE // 16])
+        gather_on_scalar(looked_up[:, SHARE:], places[:], take_list[:, SHARE // 16 :])
+        for t in range(PACK):
+            nc.tensor.matmul(
+                scores_t[:, t, :], lhsT=looked_up[:, t:I:PACK], rhs=identity[:],
+                is_transpose=True, start=False, stop=(t == PACK - 1),
+            )
+        group_values(1, nc.scalar.copy)
+        gather_on_vector(listed_values[2][:], value_pool[2][:], token_list[:])
+        turn_values(2)
+
+        weight_grouped = keep.tile([P, Q, PACK], BF16, name="weight_grouped", tag="slot2", align_bytes=64)
+        weight_codes = keep.tile([P, Q], U32, name="weight_codes", align_bytes=64)
+        weight_scales = keep.tile([P, Q], U8, name="weight_scales", align_bytes=64)
+        nc.vector.scalar_tensor_tensor(
+            out=weight_grouped[:],
+            in0=scores_t[:].rearrange("p t q -> p q t"),
+            scalar=0.0,
+            in1=slot_factor[:].unsqueeze(1).to_broadcast([P, Q, PACK]),
+            op0=ALU.max,
+            op1=ALU.mult,
+        )
+        group_values(2, nc.scalar.copy)
+        nc.vector.quantize_mx(
+            out=weight_codes[:].bitcast(FP8X4),
+            scales=weight_scales[:],
+            in_=weight_grouped[:].rearrange("p q j -> p (q j)"),
+        )
+        quantize_values(1, 2)
+
+        def multiply(first, count, dst):
+            cols = slice(first * P, (first + count) * P)
+            nc.tensor.matmul_mx(
+                out=dst,
+                lhsT=weight_codes[:].bitcast(FP8X4),
+                lhsT_scale=weight_scales[:],
+                rhs=value_codes[:, cols].bitcast(FP8X4),
+                rhs_scale=value_scales[:, cols],
+                start=True,
+                stop=True,
+            )
+
+        listed_values.append(keep.tile([P, I], BF16, name="listed_values_last", tag="listed3"))
+        gather_on_vector(listed_values[last][:, :SHARE], value_pool[last][:], token_list[:, : SHARE // 16])
+        gather_on_scalar(listed_values[last][:, SHARE:], value_pool[last][:], token_list[:, SHARE // 16 :])
+
+        early_bank = psum.tile([P, last * P], F32, name="early_bank", tag="acc0")
+        turn_values(last)
+        group_values(last, nc.scalar.copy)
+        multiply(0, 1, early_bank[:, :P])
+        multiply(1, 2, early_bank[:, P:])
+        early = keep.tile([P, last * P], F32, name="early")
+        nc.scalar.copy(early[:], early_bank[:])
+        nc.sync.dma_start(out=out[:, : last * P], in_=early[:])
+        quantize_values(last, 1)
+        late_bank = psum.tile([P, P], F32, name="late_bank", tag="acc1")
+        multiply(last, 1, late_bank[:])
+        late = keep.tile([P, P], F32, name="late")
+        nc.vector.tensor_copy(late[:], late_bank[:])
+        nc.sync.dma_start(out=out[:, last * P :], in_=late[:])

@@ -21,7 +21,7 @@ PACK = 4
 HALF = I // 2
 LIST_COLS = I // 16
 BLOCKS = E // P
-SHARE = 320
+SHARE = 288
 
 
 def tile_attend_passedthrough_read_lean_kernel(tc, query, keys_words, keys_scales, factors, vals, offs, offs2, offs3, out):
@@ -38,10 +38,10 @@ def tile_attend_passedthrough_read_lean_kernel(tc, query, keys_words, keys_scale
         def half_of(list_tile, h):
             return list_tile[:, h * LIST_COLS // 2 : (h + 1) * LIST_COLS // 2]
 
-        key_words = keep.tile([P, T], U32, name="key_words", tag="slot3", align_bytes=64)
-        key_bytes = keep.tile([P, T], U8, name="key_bytes", tag="slot2", align_bytes=64)
+        key_words = keep.tile([P, T], U32, name="key_words", tag="slot2", align_bytes=64)
+        key_bytes = keep.tile([P, T], U8, name="key_bytes", tag="slot3", align_bytes=64)
         query_raw = keep.tile([P, PACK, Q], F32, name="query_raw", tag="slot0", align_bytes=64)
-        slot_factor = keep.tile([P, PACK], F32, name="slot_factor", tag="listed3")
+        slot_factor = keep.tile([P, PACK], F32, name="slot_factor", tag="factor", align_bytes=64)
         places = keep.tile([P, Z], F32, name="places")
         identity = keep.tile([P, P], F32, name="identity")
 
@@ -57,7 +57,7 @@ def tile_attend_passedthrough_read_lean_kernel(tc, query, keys_words, keys_scale
                 out=key_bytes[r:P:32, :].bitcast(I32), in_=keys_scales[0][r:16:4, :].bitcast(I32)
             )
         nc.sync.dma_start(take_list[:], offs3)
-        nc.gpsimd.dma_start(out=slot_factor[:], in_=factors.rearrange("o (p t) -> (o p) t", t=PACK))
+        nc.scalar.dma_start(out=slot_factor[:], in_=factors.rearrange("o (p t) -> (o p) t", t=PACK))
         nc.vector.memset(places[:], 0.0)
         make_identity(nc, identity[:])
 
@@ -72,26 +72,19 @@ def tile_attend_passedthrough_read_lean_kernel(tc, query, keys_words, keys_scale
         )
 
         listed_words = keep.tile([P, I], U32, name="listed_words", align_bytes=64)
-        listed_bytes = keep.tile([P, I], U8, name="listed_bytes", align_bytes=64)
-        nc.vector.tensor_copy(listed_bytes[:], key_bytes[:].indirect(token_list[:]))
         products = keep.tile([P, I], F32, name="products")
         for h in range(2):
             cols = slice(h * HALF, (h + 1) * HALF)
+            listed_bytes = keep.tile([P, HALF], U8, name=f"listed_bytes{h}", tag="listed_bytes", align_bytes=64)
+            nc.vector.tensor_copy(listed_bytes[:], key_bytes[:].indirect(half_of(token_list, h)))
             nc.vector.tensor_copy(listed_words[:, cols], key_words[:].indirect(half_of(token_list, h)))
-        value_pool = []
-        for b in range(BLOCKS):
-            pool_block = keep.tile([P, T], F32, name=f"value_pool{b}", tag=f"slot{b}", align_bytes=64)
-            nc.sync.dma_start(out=pool_block[:], in_=vals[b * P : (b + 1) * P, :])
-            value_pool.append(pool_block)
-        for h in range(2):
-            cols = slice(h * HALF, (h + 1) * HALF)
             bank = psum.tile([P, HALF], F32, name=f"product_bank{h}", tag=f"acc{h}")
             nc.tensor.matmul_mx(
                 out=bank[:],
                 lhsT=query_codes[:].bitcast(FP8X4),
                 lhsT_scale=query_scales[:],
                 rhs=listed_words[:, cols].bitcast(FP8X4),
-                rhs_scale=listed_bytes[:, cols],
+                rhs_scale=listed_bytes[:],
                 start=True,
                 stop=True,
             )
@@ -100,6 +93,11 @@ def tile_attend_passedthrough_read_lean_kernel(tc, query, keys_words, keys_scale
             else:
                 nc.vector.tensor_copy(products[:, cols], bank[:])
             nc.scalar.activation(places[:].indirect(half_of(put_list, h)), products[:, cols], COPY)
+        value_pool = []
+        for b in range(BLOCKS):
+            pool_block = keep.tile([P, T], F32, name=f"value_pool{b}", tag=f"slot{b}", align_bytes=64)
+            nc.sync.dma_start(out=pool_block[:], in_=vals[b * P : (b + 1) * P, :])
+            value_pool.append(pool_block)
 
         scores_t = psum.tile([P, PACK, Q], F32, name="scores_t")
         for t in range(PACK):
@@ -108,103 +106,97 @@ def tile_attend_passedthrough_read_lean_kernel(tc, query, keys_words, keys_scale
                 is_transpose=True, start=(t == 0), stop=False,
             )
 
-        last = BLOCKS - 1
-        listed_values = [keep.tile([P, I], BF16, name=f"listed_values{b}", tag=f"listed{b}") for b in range(last)]
-        value_grouped = keep.tile([P, E * PACK], BF16, name="value_grouped", align_bytes=64)
-        value_codes = keep.tile([P, E], U32, name="value_codes", align_bytes=64)
-        value_scales = keep.tile([P, E], U8, name="value_scales", align_bytes=64)
-        value_banks = [psum.tile([P, 2, P], F32, name=f"value_bank{b}") for b in range(BLOCKS)]
+        listed_values = [keep.tile([P, I], BF16, name=f"listed_values{b}") for b in range(BLOCKS)]
 
-        def gather_on_vector(dst, window, offsets):
-            nc.vector.tensor_copy(dst, window.indirect(offsets))
+        def gather(dst, window, list_tile):
+            nc.vector.tensor_copy(dst[:], window[:].indirect(list_tile[:]))
 
-        def gather_on_scalar(dst, window, offsets):
-            nc.scalar.activation(dst, window.indirect(offsets), COPY)
+        def gather_shared(dst, window, list_tile):
+            nc.vector.tensor_copy(dst[:, :SHARE], window[:].indirect(list_tile[:, : SHARE // 16]))
+            nc.scalar.activation(dst[:, SHARE:], window[:].indirect(list_tile[:, SHARE // 16 :]), COPY)
 
-        def turn_values(b):
+        def turn_values(b, bank):
             words = listed_values[b][:].bitcast(F32)
             for u in range(2):
-                nc.tensor.transpose(value_banks[b][:, u, :], words[:, u : I // 2 : 2], identity[:])
+                nc.tensor.transpose(bank[:, u, :], words[:, u : I // 2 : 2], identity[:])
 
-        def group_values(b, copy):
-            copy(
-                value_grouped[:, b * P * PACK : (b + 1) * P * PACK].bitcast(F32).rearrange("p (e u) -> p e u", u=2),
-                value_banks[b][:].rearrange("p u e -> p e u"),
+        def group_values(grouped, bank):
+            nc.scalar.copy(
+                grouped[:].bitcast(F32).rearrange("p (b e u) -> p b e u", e=P, u=2),
+                bank[:].rearrange("p b u e -> p b e u"),
             )
 
-        def quantize_values(first, count):
-            cols = slice(first * P, (first + count) * P)
-            nc.vector.quantize_mx(
-                out=value_codes[:, cols].bitcast(FP8X4),
-                scales=value_scales[:, cols],
-                in_=value_grouped[:, cols.start * PACK : cols.stop * PACK],
-            )
+        def quantize(codes, scales, grouped):
+            nc.vector.quantize_mx(out=codes[:].bitcast(FP8X4), scales=scales[:], in_=grouped[:])
 
-        gather_on_vector(listed_values[0][:], value_pool[0][:], token_list[:])
-        turn_values(0)
-        group_values(0, nc.vector.tensor_copy)
-        quantize_values(0, 1)
+        pair_bank = psum.tile([P, 2, 2, P], F32, name="pair_bank")
+        for b in range(2):
+            gather(listed_values[b], value_pool[b], token_list)
+            turn_values(b, pair_bank[:, b])
 
-        gather_on_vector(listed_values[1][:], value_pool[1][:], token_list[:])
-        turn_values(1)
         looked_up = keep.tile([P, I], F32, name="looked_up", tag="slot1", align_bytes=64)
-        gather_on_vector(looked_up[:, :SHARE], places[:], take_list[:, : SHARE // 16])
-        gather_on_scalar(looked_up[:, SHARE:], places[:], take_list[:, SHARE // 16 :])
+        gather_shared(looked_up, places, take_list)
         for t in range(PACK):
             nc.tensor.matmul(
                 scores_t[:, t, :], lhsT=looked_up[:, t:I:PACK], rhs=identity[:],
                 is_transpose=True, start=False, stop=(t == PACK - 1),
             )
-        group_values(1, nc.scalar.copy)
-        gather_on_vector(listed_values[2][:], value_pool[2][:], token_list[:])
-        turn_values(2)
+        pair_grouped = keep.tile([P, 2 * P * PACK], BF16, name="pair_grouped", align_bytes=64)
+        group_values(pair_grouped, pair_bank)
 
-        weight_grouped = keep.tile([P, Q, PACK], BF16, name="weight_grouped", tag="slot2", align_bytes=64)
-        weight_codes = keep.tile([P, Q], U32, name="weight_codes", align_bytes=64)
-        weight_scales = keep.tile([P, Q], U8, name="weight_scales", align_bytes=64)
+        third_bank = psum.tile([P, 1, 2, P], F32, name="third_bank")
+        gather(listed_values[2], value_pool[2], token_list)
+        turn_values(2, third_bank[:, 0])
+
+        last_bank = psum.tile([P, 1, 2, P], F32, name="last_bank")
+        gather_shared(listed_values[3], value_pool[3], token_list)
+        turn_values(3, last_bank[:, 0])
+
+        joint_grouped = keep.tile([P, 2 * P * PACK], BF16, name="joint_grouped", tag="slot3", align_bytes=64)
+        joint_codes = keep.tile([P, 2 * P], U32, name="joint_codes", align_bytes=64)
+        joint_scales = keep.tile([P, 2 * P], U8, name="joint_scales", align_bytes=64)
+        weight_grouped, third_grouped = joint_grouped[:, : Q * PACK], joint_grouped[:, Q * PACK :]
+        weight_codes, third_codes = joint_codes[:, :Q], joint_codes[:, Q:]
+        weight_scales, third_scales = joint_scales[:, :Q], joint_scales[:, Q:]
         nc.vector.scalar_tensor_tensor(
-            out=weight_grouped[:],
+            out=weight_grouped[:].rearrange("p (q t) -> p q t", t=PACK),
             in0=scores_t[:].rearrange("p t q -> p q t"),
             scalar=0.0,
             in1=slot_factor[:].unsqueeze(1).to_broadcast([P, Q, PACK]),
             op0=ALU.max,
             op1=ALU.mult,
         )
-        group_values(2, nc.scalar.copy)
-        nc.vector.quantize_mx(
-            out=weight_codes[:].bitcast(FP8X4),
-            scales=weight_scales[:],
-            in_=weight_grouped[:].rearrange("p q j -> p (q j)"),
-        )
-        quantize_values(1, 2)
+        group_values(third_grouped, third_bank)
+        last_grouped = keep.tile([P, P * PACK], BF16, name="last_grouped", align_bytes=64)
+        group_values(last_grouped, last_bank)
+        pair_codes = keep.tile([P, 2 * P], U32, name="pair_codes", align_bytes=64)
+        pair_scales = keep.tile([P, 2 * P], U8, name="pair_scales", tag="factor", align_bytes=64)
+        quantize(pair_codes, pair_scales, pair_grouped)
+        quantize(weight_codes, weight_scales, weight_grouped)
+        quantize(third_codes, third_scales, third_grouped)
+        last_codes = keep.tile([P, P], U32, name="last_codes", align_bytes=64)
+        last_scales = keep.tile([P, P], U8, name="last_scales", align_bytes=64)
+        quantize(last_codes, last_scales, last_grouped)
 
-        def multiply(first, count, dst):
-            cols = slice(first * P, (first + count) * P)
+        def multiply(dst, codes, scales):
             nc.tensor.matmul_mx(
                 out=dst,
                 lhsT=weight_codes[:].bitcast(FP8X4),
                 lhsT_scale=weight_scales[:],
-                rhs=value_codes[:, cols].bitcast(FP8X4),
-                rhs_scale=value_scales[:, cols],
+                rhs=codes[:].bitcast(FP8X4),
+                rhs_scale=scales[:],
                 start=True,
                 stop=True,
             )
 
-        listed_values.append(keep.tile([P, I], BF16, name="listed_values_last", tag="listed3"))
-        gather_on_vector(listed_values[last][:, :SHARE], value_pool[last][:], token_list[:, : SHARE // 16])
-        gather_on_scalar(listed_values[last][:, SHARE:], value_pool[last][:], token_list[:, SHARE // 16 :])
+        def finish(first, count, codes, scales, tag, copy):
+            cols = slice(first * P, (first + count) * P)
+            bank = psum.tile([P, count * P], F32, name=f"out_bank{first}", tag=tag)
+            multiply(bank[:], codes, scales)
+            result = keep.tile([P, count * P], F32, name=f"result{first}")
+            copy(result[:], bank[:])
+            nc.sync.dma_start(out=out[:, cols], in_=result[:])
 
-        early_bank = psum.tile([P, last * P], F32, name="early_bank", tag="acc0")
-        turn_values(last)
-        group_values(last, nc.scalar.copy)
-        multiply(0, 1, early_bank[:, :P])
-        multiply(1, 2, early_bank[:, P:])
-        early = keep.tile([P, last * P], F32, name="early")
-        nc.scalar.copy(early[:], early_bank[:])
-        nc.sync.dma_start(out=out[:, : last * P], in_=early[:])
-        quantize_values(last, 1)
-        late_bank = psum.tile([P, P], F32, name="late_bank", tag="acc1")
-        multiply(last, 1, late_bank[:])
-        late = keep.tile([P, P], F32, name="late")
-        nc.vector.tensor_copy(late[:], late_bank[:])
-        nc.sync.dma_start(out=out[:, last * P :], in_=late[:])
+        finish(0, 2, pair_codes, pair_scales, "acc0", nc.scalar.copy)
+        finish(2, 1, third_codes, third_scales, "acc1", nc.scalar.copy)
+        finish(3, 1, last_codes, last_scales, "acc2", nc.vector.tensor_copy)

@@ -18,102 +18,136 @@ ALU = mybir.AluOpType
 
 P = 128
 PACK = 4
+PER_COLUMN = 16
 HALF = I // 2
-LIST_COLS = I // 16
 BLOCKS = E // P
-SHARE = 288
+VECTOR_SHARE = 288
+REGION = T * 4
 
 
-def tile_attend_passedthrough_read_lean_kernel(tc, query, keys_words, keys_scales, factors, vals, offs, offs2, offs3, out):
+def tile_attend_passedthrough_read_lean_kernel(
+    tc, query, keys_words, keys_scales, slot_factors, vals, offs, offs2, offs3, out
+):
     nc = tc.nc
     with ExitStack() as ctx:
         lists = ctx.enter_context(tc.tile_pool(name="lists", bufs=1))
         keep = ctx.enter_context(tc.tile_pool(name="keep", bufs=1))
+        regions = ctx.enter_context(tc.tile_pool(name="regions", bufs=1))
         psum = ctx.enter_context(tc.psum_pool(name="psum", bufs=1))
 
-        token_list = lists.tile([P, LIST_COLS], U16, name="token_list")
-        put_list = lists.tile([P, LIST_COLS], U16, name="put_list")
-        take_list = lists.tile([P, LIST_COLS], U16, name="take_list")
+        def region_tile(name, shape, dtype, offset):
+            return regions.tile(shape, dtype, name=name, offset=offset, align_bytes=64)
 
-        def half_of(list_tile, h):
-            return list_tile[:, h * LIST_COLS // 2 : (h + 1) * LIST_COLS // 2]
+        def mx_tile(name, shape, dtype):
+            return keep.tile(shape, dtype, name=name, align_bytes=64)
 
-        key_words = keep.tile([P, T], U32, name="key_words", tag="slot2", align_bytes=64)
-        key_bytes = keep.tile([P, T], U8, name="key_bytes", tag="slot3", align_bytes=64)
-        query_raw = keep.tile([P, PACK, Q], F32, name="query_raw", tag="slot0", align_bytes=64)
-        slot_factor = keep.tile([P, PACK], F32, name="slot_factor", tag="factor", align_bytes=64)
+        def entries(list_tile, cols):
+            return list_tile[:, cols.start // PER_COLUMN : cols.stop // PER_COLUMN]
+
+        def quantize(codes, scales, grouped):
+            nc.vector.quantize_mx(out=codes.bitcast(FP8X4), scales=scales, in_=grouped)
+
+        def multiply(bank, stationary, stationary_scales, moving, moving_scales):
+            nc.tensor.matmul_mx(
+                out=bank,
+                lhsT=stationary.bitcast(FP8X4),
+                lhsT_scale=stationary_scales,
+                rhs=moving.bitcast(FP8X4),
+                rhs_scale=moving_scales,
+                start=True,
+                stop=True,
+            )
+
+        token_list = lists.tile([P, I // PER_COLUMN], U16, name="token_list")
+        put_list = lists.tile([P, I // PER_COLUMN], U16, name="put_list")
+        take_list = lists.tile([P, I // PER_COLUMN], U16, name="take_list")
+
+        key_words = region_tile("key_words", [P, T], U32, 3 * REGION)
+        key_bytes = keep.tile([P, T], U8, name="key_bytes")
+        query_raw = region_tile("query_raw", [P, PACK, Q], F32, REGION - PACK * Q * 2)
+        slot_factor = keep.tile([P, PACK], F32, name="slot_factor")
         places = keep.tile([P, Z], F32, name="places")
         identity = keep.tile([P, P], F32, name="identity")
 
         nc.vector.memset(key_bytes[:].bitcast(I32), 0)
         nc.sync.dma_start(token_list[:], offs)
-        nc.sync.dma_start(out=query_raw[:], in_=query.rearrange("(p j) q -> p j q", j=PACK))
+        nc.sync.dma_start(out=query_raw[:], in_=query.rearrange("(p t) q -> p t q", t=PACK))
         nc.sync.dma_start(
-            out=key_words[:].bitcast(I32), in_=keys_words[0].rearrange("p n t -> p (n t)").bitcast(I32)
+            out=key_words[:].bitcast(I32), in_=keys_words[0].rearrange("p c t -> p (c t)").bitcast(I32)
         )
         nc.sync.dma_start(put_list[:], offs2)
         for r in range(4):
-            nc.scalar.dma_start(
-                out=key_bytes[r:P:32, :].bitcast(I32), in_=keys_scales[0][r:16:4, :].bitcast(I32)
-            )
+            nc.scalar.dma_start(out=key_bytes[r:P:32, :].bitcast(I32), in_=keys_scales[0][r:16:4, :].bitcast(I32))
         nc.sync.dma_start(take_list[:], offs3)
-        nc.scalar.dma_start(out=slot_factor[:], in_=factors.rearrange("o (p t) -> (o p) t", t=PACK))
+        nc.scalar.dma_start(out=slot_factor[:], in_=slot_factors.rearrange("o (p t) -> (o p) t", t=PACK))
         nc.vector.memset(places[:], 0.0)
         make_identity(nc, identity[:])
 
-        query_grouped = keep.tile([P, Q, PACK], BF16, name="query_grouped", tag="slot1", align_bytes=64)
-        query_codes = keep.tile([P, Q], U32, name="query_codes", align_bytes=64)
-        query_scales = keep.tile([P, Q], U8, name="query_scales", align_bytes=64)
-        nc.vector.tensor_copy(query_grouped[:], query_raw[:].rearrange("p j q -> p q j"))
-        nc.vector.quantize_mx(
-            out=query_codes[:].bitcast(FP8X4),
-            scales=query_scales[:],
-            in_=query_grouped[:].rearrange("p q j -> p (q j)"),
+        query_grouped = region_tile("query_grouped", [P, Q * PACK], BF16, 2 * REGION)
+        query_codes = mx_tile("query_codes", [P, Q], U32)
+        query_scales = mx_tile("query_scales", [P, Q], U8)
+        nc.vector.tensor_copy(
+            query_grouped[:].rearrange("p (q t) -> p q t", t=PACK), query_raw[:].rearrange("p t q -> p q t")
         )
+        quantize(query_codes[:], query_scales[:], query_grouped[:])
 
-        listed_words = keep.tile([P, I], U32, name="listed_words", align_bytes=64)
+        listed_words = mx_tile("listed_words", [P, I], U32)
         products = keep.tile([P, I], F32, name="products")
-        for h in range(2):
-            cols = slice(h * HALF, (h + 1) * HALF)
-            listed_bytes = keep.tile([P, HALF], U8, name=f"listed_bytes{h}", tag="listed_bytes", align_bytes=64)
-            nc.vector.tensor_copy(listed_bytes[:], key_bytes[:].indirect(half_of(token_list, h)))
-            nc.vector.tensor_copy(listed_words[:, cols], key_words[:].indirect(half_of(token_list, h)))
-            bank = psum.tile([P, HALF], F32, name=f"product_bank{h}", tag=f"acc{h}")
-            nc.tensor.matmul_mx(
-                out=bank[:],
-                lhsT=query_codes[:].bitcast(FP8X4),
-                lhsT_scale=query_scales[:],
-                rhs=listed_words[:, cols].bitcast(FP8X4),
-                rhs_scale=listed_bytes[:],
-                start=True,
-                stop=True,
-            )
-            if h == 0:
-                nc.scalar.activation(products[:, cols], bank[:], COPY)
-            else:
-                nc.vector.tensor_copy(products[:, cols], bank[:])
-            nc.scalar.activation(places[:].indirect(half_of(put_list, h)), products[:, cols], COPY)
+
+        def gather_words(cols):
+            nc.vector.tensor_copy(listed_words[:, cols], key_words[:].indirect(entries(token_list, cols)))
+
+        def gather_bytes(cols):
+            listed_bytes = keep.tile([P, HALF], U8, name="listed_bytes", align_bytes=64)
+            nc.vector.tensor_copy(listed_bytes[:], key_bytes[:].indirect(entries(token_list, cols)))
+            return listed_bytes
+
+        def copy_on_scalar(dst, src):
+            nc.scalar.activation(dst, src, COPY)
+
+        def score_and_put(piece, cols, scales, copy):
+            bank = psum.tile([P, cols.stop - cols.start], F32, name=f"product_bank{piece}", tag=f"sums{piece}")
+            multiply(bank[:], query_codes[:], query_scales[:], listed_words[:, cols], scales)
+            copy(products[:, cols], bank[:])
+            nc.scalar.activation(places[:].indirect(entries(put_list, cols)), products[:, cols], COPY)
+
+        first_bytes = gather_bytes(slice(0, HALF))
+        for piece in range(2):
+            cols = slice(piece * P, (piece + 1) * P)
+            gather_words(cols)
+            score_and_put(piece, cols, first_bytes[:, cols], copy_on_scalar)
+        second_half = slice(HALF, I)
+        gather_words(second_half)
+        second_bytes = gather_bytes(second_half)
+        score_and_put(2, second_half, second_bytes[:], nc.vector.tensor_copy)
+
         value_pool = []
         for b in range(BLOCKS):
-            pool_block = keep.tile([P, T], F32, name=f"value_pool{b}", tag=f"slot{b}", align_bytes=64)
-            nc.sync.dma_start(out=pool_block[:], in_=vals[b * P : (b + 1) * P, :])
-            value_pool.append(pool_block)
+            window = region_tile(f"value_pool{b}", [P, T], F32, b * REGION)
+            nc.sync.dma_start(out=window[:], in_=vals[b * P : (b + 1) * P, :])
+            value_pool.append(window)
 
-        scores_t = psum.tile([P, PACK, Q], F32, name="scores_t")
-        for t in range(PACK):
-            nc.tensor.matmul(
-                scores_t[:, t, :], lhsT=products[:, t:I:PACK], rhs=identity[:],
-                is_transpose=True, start=(t == 0), stop=False,
-            )
+        scores_turned = psum.tile([P, PACK, Q], F32, name="scores_turned")
+
+        def add_turned(source, opens, closes):
+            for t in range(PACK):
+                nc.tensor.matmul(
+                    scores_turned[:, t, :],
+                    lhsT=source[:, t:I:PACK],
+                    rhs=identity[:],
+                    is_transpose=True,
+                    start=opens and t == 0,
+                    stop=closes and t == PACK - 1,
+                )
+
+        add_turned(products, opens=True, closes=False)
 
         listed_values = [keep.tile([P, I], BF16, name=f"listed_values{b}") for b in range(BLOCKS)]
 
-        def gather(dst, window, list_tile):
-            nc.vector.tensor_copy(dst[:], window[:].indirect(list_tile[:]))
-
         def gather_shared(dst, window, list_tile):
-            nc.vector.tensor_copy(dst[:, :SHARE], window[:].indirect(list_tile[:, : SHARE // 16]))
-            nc.scalar.activation(dst[:, SHARE:], window[:].indirect(list_tile[:, SHARE // 16 :]), COPY)
+            first, rest = slice(0, VECTOR_SHARE), slice(VECTOR_SHARE, I)
+            nc.vector.tensor_copy(dst[:, first], window[:].indirect(entries(list_tile, first)))
+            nc.scalar.activation(dst[:, rest], window[:].indirect(entries(list_tile, rest)), COPY)
 
         def turn_values(b, bank):
             words = listed_values[b][:].bitcast(F32)
@@ -122,81 +156,63 @@ def tile_attend_passedthrough_read_lean_kernel(tc, query, keys_words, keys_scale
 
         def group_values(grouped, bank):
             nc.scalar.copy(
-                grouped[:].bitcast(F32).rearrange("p (b e u) -> p b e u", e=P, u=2),
+                grouped.bitcast(F32).rearrange("p (b e u) -> p b e u", e=P, u=2),
                 bank[:].rearrange("p b u e -> p b e u"),
             )
 
-        def quantize(codes, scales, grouped):
-            nc.vector.quantize_mx(out=codes[:].bitcast(FP8X4), scales=scales[:], in_=grouped[:])
-
         pair_bank = psum.tile([P, 2, 2, P], F32, name="pair_bank")
         for b in range(2):
-            gather(listed_values[b], value_pool[b], token_list)
+            nc.vector.tensor_copy(listed_values[b][:], value_pool[b][:].indirect(token_list[:]))
             turn_values(b, pair_bank[:, b])
 
-        looked_up = keep.tile([P, I], F32, name="looked_up", tag="slot1", align_bytes=64)
+        looked_up = region_tile("looked_up", [P, I], F32, REGION)
         gather_shared(looked_up, places, take_list)
-        for t in range(PACK):
-            nc.tensor.matmul(
-                scores_t[:, t, :], lhsT=looked_up[:, t:I:PACK], rhs=identity[:],
-                is_transpose=True, start=False, stop=(t == PACK - 1),
-            )
-        pair_grouped = keep.tile([P, 2 * P * PACK], BF16, name="pair_grouped", align_bytes=64)
-        group_values(pair_grouped, pair_bank)
+        add_turned(looked_up, opens=False, closes=True)
+        pair_grouped = mx_tile("pair_grouped", [P, 2 * P * PACK], BF16)
+        group_values(pair_grouped[:], pair_bank)
 
         third_bank = psum.tile([P, 1, 2, P], F32, name="third_bank")
-        gather(listed_values[2], value_pool[2], token_list)
+        gather_shared(listed_values[2], value_pool[2], token_list)
         turn_values(2, third_bank[:, 0])
 
         last_bank = psum.tile([P, 1, 2, P], F32, name="last_bank")
         gather_shared(listed_values[3], value_pool[3], token_list)
         turn_values(3, last_bank[:, 0])
 
-        joint_grouped = keep.tile([P, 2 * P * PACK], BF16, name="joint_grouped", tag="slot3", align_bytes=64)
-        joint_codes = keep.tile([P, 2 * P], U32, name="joint_codes", align_bytes=64)
-        joint_scales = keep.tile([P, 2 * P], U8, name="joint_scales", align_bytes=64)
-        weight_grouped, third_grouped = joint_grouped[:, : Q * PACK], joint_grouped[:, Q * PACK :]
-        weight_codes, third_codes = joint_codes[:, :Q], joint_codes[:, Q:]
-        weight_scales, third_scales = joint_scales[:, :Q], joint_scales[:, Q:]
+        operand_bytes = P * PACK * 2
+        weight_grouped = region_tile("weight_grouped", [P, Q * PACK], BF16, 3 * REGION)
+        third_grouped = region_tile("third_grouped", [P, P * PACK], BF16, 3 * REGION + operand_bytes)
+        pair_codes = region_tile("pair_codes", [P, 2 * P], U32, 3 * REGION + 2 * operand_bytes)
+
         nc.vector.scalar_tensor_tensor(
             out=weight_grouped[:].rearrange("p (q t) -> p q t", t=PACK),
-            in0=scores_t[:].rearrange("p t q -> p q t"),
+            in0=scores_turned[:].rearrange("p t q -> p q t"),
             scalar=0.0,
             in1=slot_factor[:].unsqueeze(1).to_broadcast([P, Q, PACK]),
             op0=ALU.max,
             op1=ALU.mult,
         )
-        group_values(third_grouped, third_bank)
-        last_grouped = keep.tile([P, P * PACK], BF16, name="last_grouped", align_bytes=64)
-        group_values(last_grouped, last_bank)
-        pair_codes = keep.tile([P, 2 * P], U32, name="pair_codes", align_bytes=64)
-        pair_scales = keep.tile([P, 2 * P], U8, name="pair_scales", tag="factor", align_bytes=64)
-        quantize(pair_codes, pair_scales, pair_grouped)
-        quantize(weight_codes, weight_scales, weight_grouped)
-        quantize(third_codes, third_scales, third_grouped)
-        last_codes = keep.tile([P, P], U32, name="last_codes", align_bytes=64)
-        last_scales = keep.tile([P, P], U8, name="last_scales", align_bytes=64)
-        quantize(last_codes, last_scales, last_grouped)
+        group_values(third_grouped[:], third_bank)
+        last_grouped = mx_tile("last_grouped", [P, P * PACK], BF16)
+        group_values(last_grouped[:], last_bank)
 
-        def multiply(dst, codes, scales):
-            nc.tensor.matmul_mx(
-                out=dst,
-                lhsT=weight_codes[:].bitcast(FP8X4),
-                lhsT_scale=weight_scales[:],
-                rhs=codes[:].bitcast(FP8X4),
-                rhs_scale=scales[:],
-                start=True,
-                stop=True,
-            )
+        pair_scales = mx_tile("pair_scales", [P, 2 * P], U8)
+        weight_codes, weight_scales = mx_tile("weight_codes", [P, Q], U32), mx_tile("weight_scales", [P, Q], U8)
+        third_codes, third_scales = mx_tile("third_codes", [P, P], U32), mx_tile("third_scales", [P, P], U8)
+        last_codes, last_scales = mx_tile("last_codes", [P, P], U32), mx_tile("last_scales", [P, P], U8)
+        quantize(pair_codes[:], pair_scales[:], pair_grouped[:])
+        quantize(weight_codes[:], weight_scales[:], weight_grouped[:])
+        quantize(third_codes[:], third_scales[:], third_grouped[:])
+        quantize(last_codes[:], last_scales[:], last_grouped[:])
 
-        def finish(first, count, codes, scales, tag, copy):
-            cols = slice(first * P, (first + count) * P)
-            bank = psum.tile([P, count * P], F32, name=f"out_bank{first}", tag=tag)
-            multiply(bank[:], codes, scales)
-            result = keep.tile([P, count * P], F32, name=f"result{first}")
+        def finish(piece, cols, codes, scales, copy, queue):
+            width = cols.stop - cols.start
+            bank = psum.tile([P, width], F32, name=f"out_bank{piece}", tag=f"sums{piece}")
+            multiply(bank[:], weight_codes[:], weight_scales[:], codes[:], scales[:])
+            result = keep.tile([P, width], F32, name=f"result{piece}")
             copy(result[:], bank[:])
-            nc.sync.dma_start(out=out[:, cols], in_=result[:])
+            queue.dma_start(out=out[:, cols], in_=result[:])
 
-        finish(0, 2, pair_codes, pair_scales, "acc0", nc.scalar.copy)
-        finish(2, 1, third_codes, third_scales, "acc1", nc.scalar.copy)
-        finish(3, 1, last_codes, last_scales, "acc2", nc.vector.tensor_copy)
+        finish(0, slice(0, 2 * P), pair_codes, pair_scales, nc.scalar.copy, nc.scalar)
+        finish(1, slice(2 * P, 3 * P), third_codes, third_scales, nc.vector.tensor_copy, nc.sync)
+        finish(2, slice(3 * P, E), last_codes, last_scales, nc.vector.tensor_copy, nc.sync)

from contextlib import ExitStack

import concourse.mybir as mybir
from concourse.masks import make_identity

D, T, I, Q, E, Z = 512, 2048, 512, 128, 512, 1024
FLOPS = 2 * Q * D * I + 2 * Q * I * E

F32 = mybir.dt.float32
BF16 = mybir.dt.bfloat16
I32 = mybir.dt.int32
U32 = mybir.dt.uint32
U16 = mybir.dt.uint16
U8 = mybir.dt.uint8
FP8X4 = mybir.dt.float8_e4m3fn_x4
COPY = mybir.ActivationFunctionType.Copy
ALU = mybir.AluOpType

P = 128
PACK = 4
PER_COLUMN = 16
HALF = I // 2
BLOCKS = E // P
VECTOR_SHARE = 288
REGION = T * 4


def tile_attend_passedthrough_read_lean_kernel(
    tc, query, keys_words, keys_scales, slot_factors, vals, offs, offs2, offs3, out
):
    nc = tc.nc
    with ExitStack() as ctx:
        lists = ctx.enter_context(tc.tile_pool(name="lists", bufs=1))
        keep = ctx.enter_context(tc.tile_pool(name="keep", bufs=1))
        regions = ctx.enter_context(tc.tile_pool(name="regions", bufs=1))
        psum = ctx.enter_context(tc.psum_pool(name="psum", bufs=1))

        def region_tile(name, shape, dtype, offset):
            return regions.tile(shape, dtype, name=name, offset=offset, align_bytes=64)

        def mx_tile(name, shape, dtype):
            return keep.tile(shape, dtype, name=name, align_bytes=64)

        def entries(list_tile, cols):
            return list_tile[:, cols.start // PER_COLUMN : cols.stop // PER_COLUMN]

        def quantize(codes, scales, grouped):
            nc.vector.quantize_mx(out=codes.bitcast(FP8X4), scales=scales, in_=grouped)

        def multiply(bank, stationary, stationary_scales, moving, moving_scales):
            nc.tensor.matmul_mx(
                out=bank,
                lhsT=stationary.bitcast(FP8X4),
                lhsT_scale=stationary_scales,
                rhs=moving.bitcast(FP8X4),
                rhs_scale=moving_scales,
                start=True,
                stop=True,
            )

        token_list = lists.tile([P, I // PER_COLUMN], U16, name="token_list")
        put_list = lists.tile([P, I // PER_COLUMN], U16, name="put_list")
        take_list = lists.tile([P, I // PER_COLUMN], U16, name="take_list")

        key_words = region_tile("key_words", [P, T], U32, 3 * REGION)
        key_bytes = keep.tile([P, T], U8, name="key_bytes")
        query_raw = region_tile("query_raw", [P, PACK, Q], F32, REGION - PACK * Q * 2)
        slot_factor = keep.tile([P, PACK], F32, name="slot_factor")
        places = keep.tile([P, Z], F32, name="places")
        identity = keep.tile([P, P], F32, name="identity")

        nc.vector.memset(key_bytes[:].bitcast(I32), 0)
        nc.sync.dma_start(token_list[:], offs)
        nc.sync.dma_start(out=query_raw[:], in_=query.rearrange("(p t) q -> p t q", t=PACK))
        nc.sync.dma_start(
            out=key_words[:].bitcast(I32), in_=keys_words[0].rearrange("p c t -> p (c t)").bitcast(I32)
        )
        nc.sync.dma_start(put_list[:], offs2)
        for r in range(4):
            nc.scalar.dma_start(out=key_bytes[r:P:32, :].bitcast(I32), in_=keys_scales[0][r:16:4, :].bitcast(I32))
        nc.sync.dma_start(take_list[:], offs3)
        nc.scalar.dma_start(out=slot_factor[:], in_=slot_factors.rearrange("o (p t) -> (o p) t", t=PACK))
        nc.vector.memset(places[:], 0.0)
        make_identity(nc, identity[:])

        query_grouped = region_tile("query_grouped", [P, Q * PACK], BF16, 2 * REGION)
        query_codes = mx_tile("query_codes", [P, Q], U32)
        query_scales = mx_tile("query_scales", [P, Q], U8)
        nc.vector.tensor_copy(
            query_grouped[:].rearrange("p (q t) -> p q t", t=PACK), query_raw[:].rearrange("p t q -> p q t")
        )
        quantize(query_codes[:], query_scales[:], query_grouped[:])

        listed_words = mx_tile("listed_words", [P, I], U32)
        products = keep.tile([P, I], F32, name="products")

        def gather_words(cols):
            nc.vector.tensor_copy(listed_words[:, cols], key_words[:].indirect(entries(token_list, cols)))

        def gather_bytes(cols):
            listed_bytes = keep.tile([P, HALF], U8, name="listed_bytes", align_bytes=64)
            nc.vector.tensor_copy(listed_bytes[:], key_bytes[:].indirect(entries(token_list, cols)))
            return listed_bytes

        def copy_on_scalar(dst, src):
            nc.scalar.activation(dst, src, COPY)

        def score_and_put(piece, cols, scales, copy):
            bank = psum.tile([P, cols.stop - cols.start], F32, name=f"product_bank{piece}", tag=f"sums{piece}")
            multiply(bank[:], query_codes[:], query_scales[:], listed_words[:, cols], scales)
            copy(products[:, cols], bank[:])
            nc.scalar.activation(places[:].indirect(entries(put_list, cols)), products[:, cols], COPY)

        first_bytes = gather_bytes(slice(0, HALF))
        for piece in range(2):
            cols = slice(piece * P, (piece + 1) * P)
            gather_words(cols)
            score_and_put(piece, cols, first_bytes[:, cols], copy_on_scalar)
        second_half = slice(HALF, I)
        gather_words(second_half)
        second_bytes = gather_bytes(second_half)
        score_and_put(2, second_half, second_bytes[:], nc.vector.tensor_copy)

        value_pool = []
        for b in range(BLOCKS):
            window = region_tile(f"value_pool{b}", [P, T], F32, b * REGION)
            nc.sync.dma_start(out=window[:], in_=vals[b * P : (b + 1) * P, :])
            value_pool.append(window)

        scores_turned = psum.tile([P, PACK, Q], F32, name="scores_turned")

        def add_turned(source, opens, closes):
            for t in range(PACK):
                nc.tensor.matmul(
                    scores_turned[:, t, :],
                    lhsT=source[:, t:I:PACK],
                    rhs=identity[:],
                    is_transpose=True,
                    start=opens and t == 0,
                    stop=closes and t == PACK - 1,
                )

        add_turned(products, opens=True, closes=False)

        listed_values = [keep.tile([P, I], BF16, name=f"listed_values{b}") for b in range(BLOCKS)]

        def gather_shared(dst, window, list_tile):
            first, rest = slice(0, VECTOR_SHARE), slice(VECTOR_SHARE, I)
            nc.vector.tensor_copy(dst[:, first], window[:].indirect(entries(list_tile, first)))
            nc.scalar.activation(dst[:, rest], window[:].indirect(entries(list_tile, rest)), COPY)

        def turn_values(b, bank):
            words = listed_values[b][:].bitcast(F32)
            for u in range(2):
                nc.tensor.transpose(bank[:, u, :], words[:, u : I // 2 : 2], identity[:])

        def group_values(grouped, bank):
            nc.scalar.copy(
                grouped.bitcast(F32).rearrange("p (b e u) -> p b e u", e=P, u=2),
                bank[:].rearrange("p b u e -> p b e u"),
            )

        pair_bank = psum.tile([P, 2, 2, P], F32, name="pair_bank")
        for b in range(2):
            nc.vector.tensor_copy(listed_values[b][:], value_pool[b][:].indirect(token_list[:]))
            turn_values(b, pair_bank[:, b])

        looked_up = region_tile("looked_up", [P, I], F32, REGION)
        gather_shared(looked_up, places, take_list)
        add_turned(looked_up, opens=False, closes=True)
        pair_grouped = mx_tile("pair_grouped", [P, 2 * P * PACK], BF16)
        group_values(pair_grouped[:], pair_bank)

        third_bank = psum.tile([P, 1, 2, P], F32, name="third_bank")
        gather_shared(listed_values[2], value_pool[2], token_list)
        turn_values(2, third_bank[:, 0])

        last_bank = psum.tile([P, 1, 2, P], F32, name="last_bank")
        gather_shared(listed_values[3], value_pool[3], token_list)
        turn_values(3, last_bank[:, 0])

        operand_bytes = P * PACK * 2
        weight_grouped = region_tile("weight_grouped", [P, Q * PACK], BF16, 3 * REGION)
        third_grouped = region_tile("third_grouped", [P, P * PACK], BF16, 3 * REGION + operand_bytes)
        pair_codes = region_tile("pair_codes", [P, 2 * P], U32, 3 * REGION + 2 * operand_bytes)

        nc.vector.scalar_tensor_tensor(
            out=weight_grouped[:].rearrange("p (q t) -> p q t", t=PACK),
            in0=scores_turned[:].rearrange("p t q -> p q t"),
            scalar=0.0,
            in1=slot_factor[:].unsqueeze(1).to_broadcast([P, Q, PACK]),
            op0=ALU.max,
            op1=ALU.mult,
        )
        group_values(third_grouped[:], third_bank)
        last_grouped = mx_tile("last_grouped", [P, P * PACK], BF16)
        group_values(last_grouped[:], last_bank)

        pair_scales = mx_tile("pair_scales", [P, 2 * P], U8)
        weight_codes, weight_scales = mx_tile("weight_codes", [P, Q], U32), mx_tile("weight_scales", [P, Q], U8)
        third_codes, third_scales = mx_tile("third_codes", [P, P], U32), mx_tile("third_scales", [P, P], U8)
        last_codes, last_scales = mx_tile("last_codes", [P, P], U32), mx_tile("last_scales", [P, P], U8)
        quantize(pair_codes[:], pair_scales[:], pair_grouped[:])
        quantize(weight_codes[:], weight_scales[:], weight_grouped[:])
        quantize(third_codes[:], third_scales[:], third_grouped[:])
        quantize(last_codes[:], last_scales[:], last_grouped[:])

        def finish(piece, cols, codes, scales, copy, queue):
            width = cols.stop - cols.start
            bank = psum.tile([P, width], F32, name=f"out_bank{piece}", tag=f"sums{piece}")
            multiply(bank[:], weight_codes[:], weight_scales[:], codes[:], scales[:])
            result = keep.tile([P, width], F32, name=f"result{piece}")
            copy(result[:], bank[:])
            queue.dma_start(out=out[:, cols], in_=result[:])

        finish(0, slice(0, 2 * P), pair_codes, pair_scales, nc.scalar.copy, nc.scalar)
        finish(1, slice(2 * P, 3 * P), third_codes, third_scales, nc.vector.tensor_copy, nc.sync)
        finish(2, slice(3 * P, E), last_codes, last_scales, nc.vector.tensor_copy, nc.sync)
